import numpy as np
import ml_dtypes


def mxq(x, axis, fmt="e4m3"):
    dtype, down = {"e4m3": (ml_dtypes.float8_e4m3fn, 7), "e5m2": (ml_dtypes.float8_e5m2, 14)}[fmt]
    v = np.moveaxis(np.asarray(x, np.float32).astype(ml_dtypes.bfloat16).astype(np.float64), axis, -1)
    blocks = v.reshape(v.shape[:-1] + (-1, 32))
    amax = np.abs(blocks).max(-1, keepdims=True)
    byte = np.maximum(np.where(amax > 0, np.frexp(amax)[1] - 1 + 127, 0) - down, 1)
    scale = np.exp2(byte - 127.0)
    codes = (blocks / scale).astype(np.float32).astype(dtype).astype(np.float64)
    return np.moveaxis((codes * scale).reshape(v.shape), -1, axis)


WIDE = False


def mx_kscale(k):
    if not WIDE:
        return np.ones(k)
    levels = np.array([30, -30])
    if k % 512:
        return np.exp2(np.random.permutation(np.resize(levels, k // 32))).repeat(32)
    a = np.empty((k // 512, 16))
    for p in range(k // 512):
        a[p, :8] = np.random.permutation(np.resize(levels, 8))
        for g in range(8):
            far = levels[np.abs(levels - a[p, g]) >= 10]
            a[p, g + 8] = far[np.random.randint(len(far))]
    return np.exp2(a.ravel()).repeat(32)


def f64(x):
    return np.asarray(x).astype(np.float64)


def striped(idx):
    return np.tile(np.asarray(idx).reshape(-1, 16).T, (8, 1)).astype(np.uint16)


def unstriped(offs):
    return offs[:16].T.reshape(-1).astype(np.int64)


E2M1 = np.array([0.0, 0.5, 1.0, 1.5, 2.0, 3.0, 4.0, 6.0, -0.0, -0.5, -1.0, -1.5, -2.0, -3.0, -4.0, -6.0])


def pack_weight(w, fmt):
    k, n = w.shape
    w = f64(np.asarray(w, np.float32).astype(ml_dtypes.bfloat16)).reshape(k // 32, 32, n)
    amax = np.abs(w).max(1)
    if fmt in ("e4m3", "e5m2"):
        byte = np.frexp(amax)[1] - 1 + 127 - (7 if fmt == "e4m3" else 14)
    else:
        mant, ex = np.frexp(amax / 6.0)
        byte = np.where(mant > 0.5, ex, ex - 1) + 127
    byte = np.clip(np.where(amax > 0, byte, 1), 1, 254)
    scaled = (w * np.exp2(127.0 - byte)[:, None, :]).reshape(k, n).astype(np.float32)
    by_word = np.ascontiguousarray(scaled.reshape(k // 512, 128, 4, n).transpose(0, 1, 3, 2))
    if fmt in ("e4m3", "e5m2"):
        words = by_word.astype(ml_dtypes.float8_e4m3fn if fmt == "e4m3" else ml_dtypes.float8_e5m2).view(np.uint8)
    else:
        c = by_word.astype(ml_dtypes.float4_e2m1fn).view(np.uint8) & 0xF
        words = (c[..., 0::2] | (c[..., 1::2] << 4)).reshape(k // 512, 128, 2 * n)
    return np.ascontiguousarray(words), np.ascontiguousarray(byte.astype(np.uint8).reshape(k // 512, 16, n))


def unpack_weight(words, scales, fmt):
    g, _, n = scales.shape
    words = np.ascontiguousarray(words).reshape(g, 128, n, -1)
    if fmt in ("e4m3", "e5m2"):
        vals = words.view(ml_dtypes.float8_e4m3fn if fmt == "e4m3" else ml_dtypes.float8_e5m2).astype(np.float64)
    else:
        nib = np.empty((g, 128, n, 4), np.uint8)
        nib[..., 0::2] = words & 0xF
        nib[..., 1::2] = words >> 4
        vals = E2M1[nib]
    vals = vals * np.repeat(np.exp2(scales.astype(np.float64) - 127.0), 8, axis=1)[..., None]
    return vals.transpose(0, 1, 3, 2).reshape(g * 512, n)


K, F, T, Z, J, R, C, V, O, N, S = 512, 512, 1024, 1024, 256, 512, 512, 1024, 256, 256, 1024


def setup_inputs():
    n = np.random.standard_normal
    idx = np.random.permutation(T)[:J]
    idx2 = np.random.permutation(Z)[:J]
    idx3 = np.random.permutation(C)[:J]
    idx4 = np.random.permutation(V)[:C]
    idx5 = np.random.permutation(C)[:O]
    idx6 = np.random.permutation(S)[:N]
    fk = mx_kscale(K)
    fr = mx_kscale(R)
    ff = mx_kscale(F)
    xtp = pack_weight(n((K, T)) / fk[:, None], "e5m2")
    wp = pack_weight(n((K, R)) * 1 / np.sqrt(K) * fk[:, None] * fr, "e2m1")
    xop = pack_weight(n((F, Z)) / ff[:, None], "e4m3")
    w0p = pack_weight(n((F, R)) * 1 / np.sqrt(F) * ff[:, None] * fr, "e2m1")
    vsp = pack_weight(n((R, S)) * 1 / np.sqrt(R) / fr[:, None], "e2m1")
    return {
        "xt_words": xtp[0],
        "xt_scales": xtp[1],
        "w_words": wp[0],
        "w_scales": wp[1],
        "xo_words": xop[0],
        "xo_scales": xop[1],
        "w0_words": w0p[0],
        "w0_scales": w0p[1],
        "tb": (n((R, V)) * 0.8 * fr[:, None]).astype(np.float32),
        "vs_words": vsp[0],
        "vs_scales": vsp[1],
        "offs": striped(idx),
        "offs2": striped(idx2),
        "offs3": striped(idx3),
        "offs4": striped(idx4),
        "offs5": striped(idx5),
        "offs6": striped(idx6),
    }


def reference(xt_words, xt_scales, w_words, w_scales, xo_words, xo_scales, w0_words, w0_scales, tb, vs_words, vs_scales, offs, offs2, offs3, offs4, offs5, offs6):
    idx = unstriped(offs)
    idx2 = unstriped(offs2)
    idx3 = unstriped(offs3)
    idx4 = unstriped(offs4)
    idx5 = unstriped(offs5)
    idx6 = unstriped(offs6)
    xtu = unpack_weight(xt_words, xt_scales, "e5m2")
    wu = unpack_weight(w_words, w_scales, "e2m1")
    xou = unpack_weight(xo_words, xo_scales, "e4m3")
    w0u = unpack_weight(w0_words, w0_scales, "e2m1")
    vsu = unpack_weight(vs_words, vs_scales, "e2m1")
    xtidxg = xtu[:, idx]
    xoidx2g = xou[:, idx2]
    a = wu.T @ xtidxg + w0u.T @ xoidx2g
    pw = np.zeros((R, C))
    pw[:, idx3] = a
    pg = np.abs(pw - f64(tb)[:, idx4])
    hid = pg[:, idx5]
    vsidx6g = vsu[:, idx6]
    hidq = mxq(hid, 0, "e4m3")
    y = vsidx6g.T @ hidq
    return y

@@ -1,0 +1,178 @@
+from contextlib import ExitStack
+
+import concourse.mybir as mybir
+
+K, F, T, Z, J, R, C, V, O, N, S = 512, 512, 1024, 1024, 256, 512, 512, 1024, 256, 256, 1024
+FLOPS = 2 * K * R * J + 2 * F * R * J + 2 * R * N * O
+
+F32 = mybir.dt.float32
+BF16 = mybir.dt.bfloat16
+I32 = mybir.dt.int32
+U32 = mybir.dt.uint32
+U16 = mybir.dt.uint16
+U8 = mybir.dt.uint8
+E4M3 = mybir.dt.float8_e4m3fn_x4
+E5M2 = mybir.dt.float8_e5m2_x4
+E2M1 = mybir.dt.float4_e2m1fn_x4
+ACT = mybir.ActivationFunctionType
+ALU = mybir.AluOpType
+P = 128
+PACK = 4
+
+
+def tile_list_stampedtable_bank_store_plain_kernel(
+    tc, xt_words, xt_scales, w_words, w_scales, xo_words, xo_scales, w0_words, w0_scales, tb,
+    vs_words, vs_scales, offs, offs2, offs3, offs4, offs5, offs6, out,
+):
+    nc = tc.nc
+    with ExitStack() as ctx:
+        sb = ctx.enter_context(tc.tile_pool(name="sb", bufs=1))
+        ps = ctx.enter_context(tc.psum_pool(name="ps", bufs=1))
+
+        def tile(name, shape, dtype, tag=None):
+            return sb.tile(shape, dtype, name=name, tag=tag or name, align_bytes=64)
+
+        l1 = tile("l1", [P, J // 16], U16)
+        l2 = tile("l2", [P, J // 16], U16)
+        l3 = tile("l3", [P, J // 16], U16)
+        l4 = tile("l4", [P, C // 16], U16)
+        l5 = tile("l5", [P, O // 16], U16)
+        l6 = tile("l6", [P, N // 16], U16)
+        xt_w = tile("xt_w", [P, T], U32)
+        xo_w = tile("xo_w", [P, Z], U32)
+        vs_w = tile("vs_w", [P, S], U16)
+        xt_s = tile("xt_s", [P, T], U8)
+        xo_s = tile("xo_s", [P, Z], U8)
+        vs_s = tile("vs_s", [P, S], U8)
+        w_raw = tile("w_raw", [P, 2 * R], U16)
+        ws_raw = tile("ws_raw", [P, 2 * R], U8)
+        w_p = tile("w_p", [P, 2 * R], U16)
+        ws_p = tile("ws_p", [P, 2 * R], U8)
+        tbt = [tile("tb%d" % t, [P, V], F32) for t in range(PACK)]
+        pw = [tile("pw%d" % t, [P, C], F32) for t in range(PACK)]
+        hid = tile("hid", [P, PACK, O], F32)
+        hid_bf = tile("hid_bf", [P, O, PACK], BF16)
+        hid_w = tile("hid_w", [P, O], U32)
+        hid_s = tile("hid_s", [P, O], U8)
+        xtg_w = tile("xtg_w", [P, J], U32)
+        xog_w = tile("xog_w", [P, J], U32)
+        vsg_w = tile("vsg_w", [P, N], U16)
+        xtg_s = tile("xtg_s", [P, J], U8)
+        xog_s = tile("xog_s", [P, J], U8)
+        vsg_s = tile("vsg_s", [P, N], U8)
+        y_sb = [tile("y_sb%d" % h, [P, O], F32) for h in range(2)]
+        tb_rows = tb.rearrange("(p t) v -> p t v", t=PACK)
+
+
+        def load_scales(eng, dst, src):
+            rows = src[0].bitcast(I32)
+            for q in range(4):
+                eng.dma_start(out=dst[32 * q:32 * q + 4, :].bitcast(I32), in_=rows[4 * q:4 * q + 4, :])
+
+        def words(src):
+            return src[0].rearrange("p n t -> p (n t)").bitcast(I32)
+
+        nc.vector.memset(xt_s[:].bitcast(I32), 0)
+        nc.vector.memset(ws_raw[:].bitcast(I32), 0)
+        nc.vector.memset(xo_s[:].bitcast(I32), 0)
+        nc.vector.memset(vs_s[:].bitcast(I32), 0)
+
+        nc.gpsimd.dma_start(out=xt_w[:].bitcast(I32), in_=words(xt_words))
+        nc.gpsimd.dma_start(out=xo_w[:].bitcast(I32), in_=words(xo_words))
+        for t in range(PACK):
+            nc.gpsimd.dma_start(out=tbt[t][:], in_=tb_rows[:, t, :])
+
+        nc.sync.dma_start(l1[:], offs)
+        nc.sync.dma_start(out=w_raw[:, 0:R].bitcast(I32), in_=w_words[0].bitcast(I32))
+        load_scales(nc.sync, xt_s[:], xt_scales)
+        load_scales(nc.sync, ws_raw[:, 0:R], w_scales)
+        nc.sync.dma_start(l2[:], offs2)
+        load_scales(nc.sync, xo_s[:], xo_scales)
+        nc.sync.dma_start(out=w_raw[:, R:2 * R].bitcast(I32), in_=w0_words[0].bitcast(I32))
+        load_scales(nc.sync, ws_raw[:, R:2 * R], w0_scales)
+        nc.sync.dma_start(l4[:], offs4)
+        nc.sync.dma_start(l3[:], offs3)
+        nc.sync.dma_start(l6[:], offs6)
+        nc.sync.dma_start(out=vs_w[:].bitcast(I32), in_=vs_words[0].bitcast(I32))
+        nc.sync.dma_start(l5[:], offs5)
+        load_scales(nc.sync, vs_s[:], vs_scales)
+
+        for t in range(PACK):
+            nc.gpsimd.memset(pw[t][:], 0.0)
+
+        def deal(dst, src):
+            nc.vector.tensor_copy(dst.rearrange("p (t m) -> p t m", t=PACK), src.rearrange("p (m t) -> p t m", t=PACK))
+
+        nc.vector.tensor_copy(xtg_w[:], xt_w[:].indirect(l1[:]))
+        deal(w_p[:, 0:R], w_raw[:, 0:R])
+        nc.vector.tensor_copy(xtg_s[:], xt_s[:].indirect(l1[:]))
+        deal(ws_p[:, 0:R], ws_raw[:, 0:R])
+        nc.vector.tensor_copy(xog_w[:], xo_w[:].indirect(l2[:]))
+        nc.vector.tensor_copy(xog_s[:], xo_s[:].indirect(l2[:]))
+        deal(w_p[:, R:2 * R], w_raw[:, R:2 * R])
+        deal(ws_p[:, R:2 * R], ws_raw[:, R:2 * R])
+
+        acc = [ps.tile([P, J], F32, name="acc%d" % t) for t in range(PACK)]
+        for t in range(PACK):
+            c0 = slice(t * P, (t + 1) * P)
+            nc.tensor.matmul_mx(out=acc[t][:], lhsT=w_p[:, c0].bitcast(E2M1), lhsT_scale=ws_p[:, c0],
+                                rhs=xtg_w[:].bitcast(E5M2), rhs_scale=xtg_s[:], start=True, stop=False)
+        for t in range(PACK):
+            c1 = slice(R + t * P, R + (t + 1) * P)
+            nc.tensor.matmul_mx(out=acc[t][:], lhsT=w_p[:, c1].bitcast(E2M1), lhsT_scale=ws_p[:, c1],
+                                rhs=xog_w[:].bitcast(E4M3), rhs_scale=xog_s[:], start=False, stop=True)
+
+
+        tbg0 = tile("tbg0", [P, C], F32)
+        tbg1 = tile("tbg1", [P, C], F32)
+        nc.scalar.activation(tbg0[:], tbt[0][:].indirect(l4[:]), ACT.Copy)
+        nc.scalar.activation(tbg1[:], tbt[1][:].indirect(l4[:]), ACT.Copy)
+
+        a0 = tile("a0", [P, J], F32, tag="stage_v")
+        a1 = tile("a1", [P, J], F32, tag="stage_s")
+        a2 = tile("a2", [P, J], F32)
+        a3 = tile("a3", [P, J], F32)
+        nc.vector.tensor_copy(a0[:], acc[0][:])
+        nc.scalar.copy(a1[:], acc[1][:])
+        nc.vector.tensor_copy(pw[0][:].indirect(l3[:]), a0[:])
+        nc.scalar.activation(pw[1][:].indirect(l3[:]), a1[:], ACT.Copy)
+        nc.vector.tensor_copy(a2[:], acc[2][:])
+        nc.scalar.copy(a3[:], acc[3][:])
+        tbg2 = tile("tbg2", [P, C], F32, tag="stage_v")
+        tbg3 = tile("tbg3", [P, C], F32, tag="stage_s")
+        nc.vector.tensor_copy(tbg2[:], tbt[2][:].indirect(l4[:]))
+        nc.scalar.activation(tbg3[:], tbt[3][:].indirect(l4[:]), ACT.Copy)
+        nc.vector.tensor_copy(pw[2][:].indirect(l3[:]), a2[:])
+        nc.scalar.activation(pw[3][:].indirect(l3[:]), a3[:], ACT.Copy)
+        tbg = [tbg0, tbg1, tbg2, tbg3]
+
+        dif = [tile("dif%d" % t, [P, C], F32) for t in range(PACK)]
+        for t in range(3):
+            nc.gpsimd.tensor_tensor(dif[t][:], pw[t][:], tbg[t][:], ALU.subtract)
+        nc.vector.tensor_copy(vsg_w[:], vs_w[:].indirect(l6[:]))
+        nc.vector.tensor_tensor(dif[3][:], pw[3][:], tbg[3][:], ALU.subtract)
+        pg = {}
+        for t in (0, 1, 3, 2):
+            pg[t] = tile("pg%d" % t, [P, C], F32, tag="dif1" if t == 3 else None)
+            nc.scalar.activation(pg[t][:], dif[t][:], ACT.Abs)
+        for t in (0, 1):
+            nc.vector.tensor_copy(hid[:, t, :], pg[t][:].indirect(l5[:]))
+        nc.vector.tensor_copy(vsg_s[:], vs_s[:].indirect(l6[:]))
+        nc.vector.tensor_copy(hid[:, 3, :], pg[3][:].indirect(l5[:]))
+        nc.scalar.activation(hid[:, 2, :], pg[2][:].indirect(l5[:]), ACT.Copy)
+
+        nc.vector.tensor_copy(hid_bf[:].rearrange("p (c i) t -> p c t i", i=4),
+                              hid[:].rearrange("p t (c i) -> p c t i", i=4))
+        nc.vector.quantize_mx(out=hid_w[:].bitcast(E4M3), scales=hid_s[:],
+                              in_=hid_bf[:].rearrange("p o t -> p (o t)"))
+        for h in range(2):
+            cols = slice(h * P, (h + 1) * P)
+            y = ps.tile([P, O], F32, name="y%d" % h)
+            nc.tensor.matmul_mx(out=y[:], lhsT=vsg_w[:, cols].bitcast(E2M1), lhsT_scale=vsg_s[:, cols],
+                                rhs=hid_w[:].bitcast(E4M3), rhs_scale=hid_s[:], start=True, stop=True)
+            if h == 0:
+                nc.vector.tensor_copy(y_sb[h][:], y[:])
+                nc.sync.dma_start(out=out[cols, :], in_=y_sb[h][:])
+            else:
+                nc.scalar.copy(y_sb[h][:], y[:])
+                nc.scalar.dma_start(out=out[cols, :], in_=y_sb[h][:])

@@ -64,53 +64,52 @@ def tile_list_stampedtable_bank_store_plain_kernel(
         tb_rows = tb.rearrange("(p t) v -> p t v", t=PACK)
 
 
-        def load_scales(eng, dst, src):
+        def load_scale_rows(dst, src, quadrants):
             rows = src[0].bitcast(I32)
-            for q in range(4):
-                eng.dma_start(out=dst[32 * q:32 * q + 4, :].bitcast(I32), in_=rows[4 * q:4 * q + 4, :])
+            for q in quadrants:
+                nc.sync.dma_start(out=dst[32 * q:32 * q + 4, :].bitcast(I32), in_=rows[4 * q:4 * q + 4, :])
 
         def words(src):
             return src[0].rearrange("p n t -> p (n t)").bitcast(I32)
 
-        nc.vector.memset(xt_s[:].bitcast(I32), 0)
         nc.vector.memset(ws_raw[:].bitcast(I32), 0)
+        nc.vector.memset(xt_s[:].bitcast(I32), 0)
         nc.vector.memset(xo_s[:].bitcast(I32), 0)
         nc.vector.memset(vs_s[:].bitcast(I32), 0)
-
-        nc.gpsimd.dma_start(out=xt_w[:].bitcast(I32), in_=words(xt_words))
-        nc.gpsimd.dma_start(out=xo_w[:].bitcast(I32), in_=words(xo_words))
         for t in range(PACK):
-            nc.gpsimd.dma_start(out=tbt[t][:], in_=tb_rows[:, t, :])
+            nc.vector.memset(pw[t][:], 0.0)
 
-        nc.sync.dma_start(l1[:], offs)
         nc.sync.dma_start(out=w_raw[:, 0:R].bitcast(I32), in_=w_words[0].bitcast(I32))
-        load_scales(nc.sync, xt_s[:], xt_scales)
-        load_scales(nc.sync, ws_raw[:, 0:R], w_scales)
-        nc.sync.dma_start(l2[:], offs2)
-        load_scales(nc.sync, xo_s[:], xo_scales)
+        load_scale_rows(ws_raw[:, 0:R], w_scales, range(4))
         nc.sync.dma_start(out=w_raw[:, R:2 * R].bitcast(I32), in_=w0_words[0].bitcast(I32))
-        load_scales(nc.sync, ws_raw[:, R:2 * R], w0_scales)
-        nc.sync.dma_start(l4[:], offs4)
+        nc.sync.dma_start(l1[:], offs)
+        nc.sync.dma_start(out=xt_w[:].bitcast(I32), in_=words(xt_words))
+        load_scale_rows(xt_s[:], xt_scales, range(4))
+        nc.sync.dma_start(l2[:], offs2)
+        load_scale_rows(ws_raw[:, R:2 * R], w0_scales, range(1))
+        nc.sync.dma_start(out=xo_w[:].bitcast(I32), in_=words(xo_words))
+        load_scale_rows(ws_raw[:, R:2 * R], w0_scales, range(1, 4))
+        load_scale_rows(xo_s[:], xo_scales, range(4))
         nc.sync.dma_start(l3[:], offs3)
+        nc.sync.dma_start(l4[:], offs4)
+        for t in range(PACK):
+            nc.sync.dma_start(out=tbt[t][:], in_=tb_rows[:, t, :])
+        load_scale_rows(vs_s[:], vs_scales, range(4))
         nc.sync.dma_start(l6[:], offs6)
         nc.sync.dma_start(out=vs_w[:].bitcast(I32), in_=vs_words[0].bitcast(I32))
         nc.sync.dma_start(l5[:], offs5)
-        load_scales(nc.sync, vs_s[:], vs_scales)
-
-        for t in range(PACK):
-            nc.gpsimd.memset(pw[t][:], 0.0)
 
         def deal(dst, src):
             nc.vector.tensor_copy(dst.rearrange("p (t m) -> p t m", t=PACK), src.rearrange("p (m t) -> p t m", t=PACK))
 
-        nc.vector.tensor_copy(xtg_w[:], xt_w[:].indirect(l1[:]))
         deal(w_p[:, 0:R], w_raw[:, 0:R])
-        nc.vector.tensor_copy(xtg_s[:], xt_s[:].indirect(l1[:]))
         deal(ws_p[:, 0:R], ws_raw[:, 0:R])
-        nc.vector.tensor_copy(xog_w[:], xo_w[:].indirect(l2[:]))
-        nc.vector.tensor_copy(xog_s[:], xo_s[:].indirect(l2[:]))
         deal(w_p[:, R:2 * R], w_raw[:, R:2 * R])
+        nc.vector.tensor_copy(xtg_w[:], xt_w[:].indirect(l1[:]))
+        nc.vector.tensor_copy(xtg_s[:], xt_s[:].indirect(l1[:]))
+        nc.vector.tensor_copy(xog_w[:], xo_w[:].indirect(l2[:]))
         deal(ws_p[:, R:2 * R], ws_raw[:, R:2 * R])
+        nc.vector.tensor_copy(xog_s[:], xo_s[:].indirect(l2[:]))
 
         acc = [ps.tile([P, J], F32, name="acc%d" % t) for t in range(PACK)]
         for t in range(PACK):
@@ -123,46 +122,42 @@ def tile_list_stampedtable_bank_store_plain_kernel(
                                 rhs=xog_w[:].bitcast(E4M3), rhs_scale=xog_s[:], start=False, stop=True)
 
 
-        tbg0 = tile("tbg0", [P, C], F32)
-        tbg1 = tile("tbg1", [P, C], F32)
-        nc.scalar.activation(tbg0[:], tbt[0][:].indirect(l4[:]), ACT.Copy)
-        nc.scalar.activation(tbg1[:], tbt[1][:].indirect(l4[:]), ACT.Copy)
-
-        a0 = tile("a0", [P, J], F32, tag="stage_v")
-        a1 = tile("a1", [P, J], F32, tag="stage_s")
-        a2 = tile("a2", [P, J], F32)
-        a3 = tile("a3", [P, J], F32)
-        nc.vector.tensor_copy(a0[:], acc[0][:])
-        nc.scalar.copy(a1[:], acc[1][:])
-        nc.vector.tensor_copy(pw[0][:].indirect(l3[:]), a0[:])
-        nc.scalar.activation(pw[1][:].indirect(l3[:]), a1[:], ACT.Copy)
-        nc.vector.tensor_copy(a2[:], acc[2][:])
-        nc.scalar.copy(a3[:], acc[3][:])
-        tbg2 = tile("tbg2", [P, C], F32, tag="stage_v")
-        tbg3 = tile("tbg3", [P, C], F32, tag="stage_s")
-        nc.vector.tensor_copy(tbg2[:], tbt[2][:].indirect(l4[:]))
-        nc.scalar.activation(tbg3[:], tbt[3][:].indirect(l4[:]), ACT.Copy)
-        nc.vector.tensor_copy(pw[2][:].indirect(l3[:]), a2[:])
-        nc.scalar.activation(pw[3][:].indirect(l3[:]), a3[:], ACT.Copy)
-        tbg = [tbg0, tbg1, tbg2, tbg3]
+        a_sb = [tile("a_sb%d" % t, [P, J], F32) for t in range(PACK)]
+        for t in range(PACK):
+            if t % 2 == 0:
+                nc.vector.tensor_copy(a_sb[t][:], acc[t][:])
+            else:
+                nc.scalar.copy(a_sb[t][:], acc[t][:])
+        for t in range(PACK):
+            if t % 2 == 0:
+                nc.vector.tensor_copy(pw[t][:].indirect(l3[:]), a_sb[t][:])
+            else:
+                nc.scalar.activation(pw[t][:].indirect(l3[:]), a_sb[t][:], ACT.Copy)
 
         dif = [tile("dif%d" % t, [P, C], F32) for t in range(PACK)]
-        for t in range(3):
-            nc.gpsimd.tensor_tensor(dif[t][:], pw[t][:], tbg[t][:], ALU.subtract)
-        nc.vector.tensor_copy(vsg_w[:], vs_w[:].indirect(l6[:]))
-        nc.vector.tensor_tensor(dif[3][:], pw[3][:], tbg[3][:], ALU.subtract)
-        pg = {}
-        for t in (0, 1, 3, 2):
-            pg[t] = tile("pg%d" % t, [P, C], F32, tag="dif1" if t == 3 else None)
+        for t in range(PACK):
+            if t % 2 == 0:
+                nc.vector.tensor_tensor(dif[t][:], tbt[t][:].indirect(l4[:]), pw[t][:], ALU.subtract)
+            else:
+                tbg = tile("tbg%d" % t, [P, C], F32)
+                nc.scalar.activation(tbg[:], tbt[t][:].indirect(l4[:]), ACT.Copy)
+                nc.vector.tensor_tensor(dif[t][:], tbg[:], pw[t][:], ALU.subtract)
+        pg = []
+        for t in range(PACK):
+            pg.append(tile("pg%d" % t, [P, C], F32, tag="tb3" if t == 0 else None))
             nc.scalar.activation(pg[t][:], dif[t][:], ACT.Abs)
-        for t in (0, 1):
-            nc.vector.tensor_copy(hid[:, t, :], pg[t][:].indirect(l5[:]))
         nc.vector.tensor_copy(vsg_s[:], vs_s[:].indirect(l6[:]))
-        nc.vector.tensor_copy(hid[:, 3, :], pg[3][:].indirect(l5[:]))
-        nc.scalar.activation(hid[:, 2, :], pg[2][:].indirect(l5[:]), ACT.Copy)
+        nc.vector.tensor_copy(vsg_w[:], vs_w[:].indirect(l6[:]))
+        for t in (0, 1, 3):
+            nc.scalar.activation(hid[:, t, :], pg[t][:].indirect(l5[:]), ACT.Copy)
+        for t in (2,):
+            nc.vector.tensor_copy(hid[:, t, :], pg[t][:].indirect(l5[:]))
 
-        nc.vector.tensor_copy(hid_bf[:].rearrange("p (c i) t -> p c t i", i=4),
-                              hid[:].rearrange("p t (c i) -> p c t i", i=4))
+        half = O // 2
+        nc.vector.tensor_copy(hid_bf[:, 0:half, :].rearrange("p (c i) t -> p c t i", i=4),
+                              hid[:, :, 0:half].rearrange("p t (c i) -> p c t i", i=4))
+        nc.scalar.copy(hid_bf[:, half:O, :].rearrange("p (c i) t -> p c t i", i=4),
+                       hid[:, :, half:O].rearrange("p t (c i) -> p c t i", i=4))
         nc.vector.quantize_mx(out=hid_w[:].bitcast(E4M3), scales=hid_s[:],
                               in_=hid_bf[:].rearrange("p o t -> p (o t)"))
         for h in range(2):

@@ -51,16 +51,12 @@ def tile_list_stampedtable_bank_store_plain_kernel(
         tbt = [tile("tb%d" % t, [P, V], F32) for t in range(PACK)]
         pw = [tile("pw%d" % t, [P, C], F32) for t in range(PACK)]
         hid = tile("hid", [P, PACK, O], F32)
-        hid_bf = tile("hid_bf", [P, O, PACK], BF16)
-        hid_w = tile("hid_w", [P, O], U32)
-        hid_s = tile("hid_s", [P, O], U8)
         xtg_w = tile("xtg_w", [P, J], U32)
         xog_w = tile("xog_w", [P, J], U32)
         vsg_w = tile("vsg_w", [P, N], U16)
         xtg_s = tile("xtg_s", [P, J], U8)
         xog_s = tile("xog_s", [P, J], U8)
         vsg_s = tile("vsg_s", [P, N], U8)
-        y_sb = [tile("y_sb%d" % h, [P, O], F32) for h in range(2)]
         tb_rows = tb.rearrange("(p t) v -> p t v", t=PACK)
 
 
@@ -92,12 +88,12 @@ def tile_list_stampedtable_bank_store_plain_kernel(
         load_scale_rows(xo_s[:], xo_scales, range(4))
         nc.sync.dma_start(l3[:], offs3)
         nc.sync.dma_start(l4[:], offs4)
-        for t in range(PACK):
-            nc.sync.dma_start(out=tbt[t][:], in_=tb_rows[:, t, :])
         load_scale_rows(vs_s[:], vs_scales, range(4))
         nc.sync.dma_start(l6[:], offs6)
-        nc.sync.dma_start(out=vs_w[:].bitcast(I32), in_=vs_words[0].bitcast(I32))
+        for t in range(PACK):
+            nc.sync.dma_start(out=tbt[t][:], in_=tb_rows[:, t, :])
         nc.sync.dma_start(l5[:], offs5)
+        nc.sync.dma_start(out=vs_w[:].bitcast(I32), in_=vs_words[0].bitcast(I32))
 
         def deal(dst, src):
             nc.vector.tensor_copy(dst.rearrange("p (t m) -> p t m", t=PACK), src.rearrange("p (m t) -> p t m", t=PACK))
@@ -128,46 +124,43 @@ def tile_list_stampedtable_bank_store_plain_kernel(
                 nc.vector.tensor_copy(a_sb[t][:], acc[t][:])
             else:
                 nc.scalar.copy(a_sb[t][:], acc[t][:])
-        for t in range(PACK):
-            if t % 2 == 0:
-                nc.vector.tensor_copy(pw[t][:].indirect(l3[:]), a_sb[t][:])
-            else:
-                nc.scalar.activation(pw[t][:].indirect(l3[:]), a_sb[t][:], ACT.Copy)
+        nc.vector.tensor_copy(pw[0][:].indirect(l3[:]), a_sb[0][:])
+        for t in range(1, PACK):
+            nc.scalar.activation(pw[t][:].indirect(l3[:]), a_sb[t][:], ACT.Copy)
+        nc.vector.tensor_copy(vsg_s[:], vs_s[:].indirect(l6[:]))
 
         dif = [tile("dif%d" % t, [P, C], F32) for t in range(PACK)]
+        pg = [tile("pg%d" % t, [P, C], F32) for t in range(PACK)]
         for t in range(PACK):
-            if t % 2 == 0:
-                nc.vector.tensor_tensor(dif[t][:], tbt[t][:].indirect(l4[:]), pw[t][:], ALU.subtract)
-            else:
-                tbg = tile("tbg%d" % t, [P, C], F32)
-                nc.scalar.activation(tbg[:], tbt[t][:].indirect(l4[:]), ACT.Copy)
-                nc.vector.tensor_tensor(dif[t][:], tbg[:], pw[t][:], ALU.subtract)
-        pg = []
-        for t in range(PACK):
-            pg.append(tile("pg%d" % t, [P, C], F32, tag="tb3" if t == 0 else None))
-            nc.scalar.activation(pg[t][:], dif[t][:], ACT.Abs)
-        nc.vector.tensor_copy(vsg_s[:], vs_s[:].indirect(l6[:]))
+            nc.vector.tensor_tensor(dif[t][:], tbt[t][:].indirect(l4[:]), pw[t][:], ALU.subtract)
         nc.vector.tensor_copy(vsg_w[:], vs_w[:].indirect(l6[:]))
-        for t in (0, 1, 3):
-            nc.scalar.activation(hid[:, t, :], pg[t][:].indirect(l5[:]), ACT.Copy)
-        for t in (2,):
+        for t in range(PACK - 1):
+            nc.scalar.activation(pg[t][:], dif[t][:], ACT.Abs)
+        nc.scalar.activation(hid[:, 0, :], pg[0][:].indirect(l5[:]), ACT.Copy)
+        nc.scalar.activation(pg[3][:], dif[3][:], ACT.Abs)
+        nc.scalar.activation(hid[:, 1, :], pg[1][:].indirect(l5[:]), ACT.Copy)
+        for t in (2, 3):
             nc.vector.tensor_copy(hid[:, t, :], pg[t][:].indirect(l5[:]))
 
-        half = O // 2
-        nc.vector.tensor_copy(hid_bf[:, 0:half, :].rearrange("p (c i) t -> p c t i", i=4),
-                              hid[:, :, 0:half].rearrange("p t (c i) -> p c t i", i=4))
-        nc.scalar.copy(hid_bf[:, half:O, :].rearrange("p (c i) t -> p c t i", i=4),
-                       hid[:, :, half:O].rearrange("p t (c i) -> p c t i", i=4))
-        nc.vector.quantize_mx(out=hid_w[:].bitcast(E4M3), scales=hid_s[:],
-                              in_=hid_bf[:].rearrange("p o t -> p (o t)"))
-        for h in range(2):
-            cols = slice(h * P, (h + 1) * P)
-            y = ps.tile([P, O], F32, name="y%d" % h)
-            nc.tensor.matmul_mx(out=y[:], lhsT=vsg_w[:, cols].bitcast(E2M1), lhsT_scale=vsg_s[:, cols],
-                                rhs=hid_w[:].bitcast(E4M3), rhs_scale=hid_s[:], start=True, stop=True)
-            if h == 0:
-                nc.vector.tensor_copy(y_sb[h][:], y[:])
-                nc.sync.dma_start(out=out[cols, :], in_=y_sb[h][:])
-            else:
-                nc.scalar.copy(y_sb[h][:], y[:])
-                nc.scalar.dma_start(out=out[cols, :], in_=y_sb[h][:])
+        hid_bf = [tile("hid_bf%d" % g, [P, P, PACK], BF16) for g in range(2)]
+        hid_w = [tile("hid_w%d" % g, [P, P], U32) for g in range(2)]
+        hid_s = [tile("hid_s%d" % g, [P, P], U8) for g in range(2)]
+        for g in range(2):
+            nc.vector.tensor_copy(hid_bf[g][:].rearrange("p (c i) t -> p c t i", i=4),
+                                  hid[:, :, g * P:(g + 1) * P].rearrange("p t (c i) -> p c t i", i=4))
+        for g in range(2):
+            nc.vector.quantize_mx(out=hid_w[g][:].bitcast(E4M3), scales=hid_s[g][:],
+                                  in_=hid_bf[g][:].rearrange("p o t -> p (o t)"))
+        for g in range(2):
+            for h in range(2):
+                rows = slice(h * P, (h + 1) * P)
+                y = ps.tile([P, P], F32, name="y%d%d" % (g, h))
+                nc.tensor.matmul_mx(out=y[:], lhsT=vsg_w[:, rows].bitcast(E2M1), lhsT_scale=vsg_s[:, rows],
+                                    rhs=hid_w[g][:].bitcast(E4M3), rhs_scale=hid_s[g][:], start=True, stop=True)
+                y_sb = tile("y_sb%d%d" % (g, h), [P, P], F32)
+                if g == 1 and h == 0:
+                    nc.vector.tensor_copy(y_sb[:], y[:])
+                else:
+                    nc.scalar.copy(y_sb[:], y[:])
+                queue = nc.scalar if g == 1 and h == 1 else nc.sync
+                queue.dma_start(out=out[rows, g * P:(g + 1) * P], in_=y_sb[:])

@@ -120,7 +120,7 @@ def tile_list_stampedtable_bank_store_plain_kernel(
 
         a_sb = [tile("a_sb%d" % t, [P, J], F32) for t in range(PACK)]
         for t in range(PACK):
-            if t % 2 == 0:
+            if t == 0:
                 nc.vector.tensor_copy(a_sb[t][:], acc[t][:])
             else:
                 nc.scalar.copy(a_sb[t][:], acc[t][:])
@@ -131,16 +131,19 @@ def tile_list_stampedtable_bank_store_plain_kernel(
 
         dif = [tile("dif%d" % t, [P, C], F32) for t in range(PACK)]
         pg = [tile("pg%d" % t, [P, C], F32) for t in range(PACK)]
-        for t in range(PACK):
-            nc.vector.tensor_tensor(dif[t][:], tbt[t][:].indirect(l4[:]), pw[t][:], ALU.subtract)
-        nc.vector.tensor_copy(vsg_w[:], vs_w[:].indirect(l6[:]))
         for t in range(PACK - 1):
+            nc.vector.tensor_tensor(dif[t][:], tbt[t][:].indirect(l4[:]), pw[t][:], ALU.subtract)
             nc.scalar.activation(pg[t][:], dif[t][:], ACT.Abs)
-        nc.scalar.activation(hid[:, 0, :], pg[0][:].indirect(l5[:]), ACT.Copy)
-        nc.scalar.activation(pg[3][:], dif[3][:], ACT.Abs)
-        nc.scalar.activation(hid[:, 1, :], pg[1][:].indirect(l5[:]), ACT.Copy)
-        for t in (2, 3):
-            nc.vector.tensor_copy(hid[:, t, :], pg[t][:].indirect(l5[:]))
+        for g in range(2):
+            cols = slice(g * C // 2, (g + 1) * C // 2)
+            nc.vector.tensor_tensor(dif[3][:, cols], tbt[3][:].indirect(l4[:, 16 * g:16 * g + 16]), pw[3][:, cols], ALU.subtract)
+            nc.scalar.activation(pg[3][:, cols], dif[3][:, cols], ACT.Abs)
+        nc.vector.tensor_copy(vsg_w[:], vs_w[:].indirect(l6[:]))
+        for t in (0, 1):
+            nc.scalar.activation(hid[:, t, :], pg[t][:].indirect(l5[:]), ACT.Copy)
+        nc.vector.tensor_copy(hid[:, 2, :], pg[2][:].indirect(l5[:]))
+        nc.vector.tensor_copy(hid[:, 3, 0:P], pg[3][:].indirect(l5[:, 0:8]))
+        nc.scalar.activation(hid[:, 3, P:O], pg[3][:].indirect(l5[:, 8:16]), ACT.Copy)
 
         hid_bf = [tile("hid_bf%d" % g, [P, P, PACK], BF16) for g in range(2)]
         hid_w = [tile("hid_w%d" % g, [P, P], U32) for g in range(2)]

from contextlib import ExitStack

import concourse.mybir as mybir

K, F, T, Z, J, R, C, V, O, N, S = 512, 512, 1024, 1024, 256, 512, 512, 1024, 256, 256, 1024
FLOPS = 2 * K * R * J + 2 * F * R * J + 2 * R * N * O

F32 = mybir.dt.float32
BF16 = mybir.dt.bfloat16
I32 = mybir.dt.int32
U32 = mybir.dt.uint32
U16 = mybir.dt.uint16
U8 = mybir.dt.uint8
E4M3 = mybir.dt.float8_e4m3fn_x4
E5M2 = mybir.dt.float8_e5m2_x4
E2M1 = mybir.dt.float4_e2m1fn_x4
ACT = mybir.ActivationFunctionType
ALU = mybir.AluOpType
P = 128
PACK = 4


def tile_list_stampedtable_bank_store_plain_kernel(
    tc, xt_words, xt_scales, w_words, w_scales, xo_words, xo_scales, w0_words, w0_scales, tb,
    vs_words, vs_scales, offs, offs2, offs3, offs4, offs5, offs6, out,
):
    nc = tc.nc
    with ExitStack() as ctx:
        sb = ctx.enter_context(tc.tile_pool(name="sb", bufs=1))
        ps = ctx.enter_context(tc.psum_pool(name="ps", bufs=1))

        def tile(name, shape, dtype, tag=None):
            return sb.tile(shape, dtype, name=name, tag=tag or name, align_bytes=64)

        l1 = tile("l1", [P, J // 16], U16)
        l2 = tile("l2", [P, J // 16], U16)
        l3 = tile("l3", [P, J // 16], U16)
        l4 = tile("l4", [P, C // 16], U16)
        l5 = tile("l5", [P, O // 16], U16)
        l6 = tile("l6", [P, N // 16], U16)
        xt_w = tile("xt_w", [P, T], U32)
        xo_w = tile("xo_w", [P, Z], U32)
        vs_w = tile("vs_w", [P, S], U16)
        xt_s = tile("xt_s", [P, T], U8)
        xo_s = tile("xo_s", [P, Z], U8)
        vs_s = tile("vs_s", [P, S], U8)
        w_raw = tile("w_raw", [P, 2 * R], U16)
        ws_raw = tile("ws_raw", [P, 2 * R], U8)
        w_p = tile("w_p", [P, 2 * R], U16)
        ws_p = tile("ws_p", [P, 2 * R], U8)
        tbt = [tile("tb%d" % t, [P, V], F32) for t in range(PACK)]
        pw = [tile("pw%d" % t, [P, C], F32) for t in range(PACK)]
        hid = tile("hid", [P, PACK, O], F32)
        xtg_w = tile("xtg_w", [P, J], U32)
        xog_w = tile("xog_w", [P, J], U32)
        vsg_w = tile("vsg_w", [P, N], U16)
        xtg_s = tile("xtg_s", [P, J], U8)
        xog_s = tile("xog_s", [P, J], U8)
        vsg_s = tile("vsg_s", [P, N], U8)
        tb_rows = tb.rearrange("(p t) v -> p t v", t=PACK)


        def load_scale_rows(dst, src, quadrants):
            rows = src[0].bitcast(I32)
            for q in quadrants:
                nc.sync.dma_start(out=dst[32 * q:32 * q + 4, :].bitcast(I32), in_=rows[4 * q:4 * q + 4, :])

        def words(src):
            return src[0].rearrange("p n t -> p (n t)").bitcast(I32)

        nc.vector.memset(ws_raw[:].bitcast(I32), 0)
        nc.vector.memset(xt_s[:].bitcast(I32), 0)
        nc.vector.memset(xo_s[:].bitcast(I32), 0)
        nc.vector.memset(vs_s[:].bitcast(I32), 0)
        for t in range(PACK):
            nc.vector.memset(pw[t][:], 0.0)

        nc.sync.dma_start(out=w_raw[:, 0:R].bitcast(I32), in_=w_words[0].bitcast(I32))
        load_scale_rows(ws_raw[:, 0:R], w_scales, range(4))
        nc.sync.dma_start(out=w_raw[:, R:2 * R].bitcast(I32), in_=w0_words[0].bitcast(I32))
        nc.sync.dma_start(l1[:], offs)
        nc.sync.dma_start(out=xt_w[:].bitcast(I32), in_=words(xt_words))
        load_scale_rows(xt_s[:], xt_scales, range(4))
        nc.sync.dma_start(l2[:], offs2)
        load_scale_rows(ws_raw[:, R:2 * R], w0_scales, range(1))
        nc.sync.dma_start(out=xo_w[:].bitcast(I32), in_=words(xo_words))
        load_scale_rows(ws_raw[:, R:2 * R], w0_scales, range(1, 4))
        load_scale_rows(xo_s[:], xo_scales, range(4))
        nc.sync.dma_start(l3[:], offs3)
        nc.sync.dma_start(l4[:], offs4)
        load_scale_rows(vs_s[:], vs_scales, range(4))
        nc.sync.dma_start(l6[:], offs6)
        for t in range(PACK):
            nc.sync.dma_start(out=tbt[t][:], in_=tb_rows[:, t, :])
        nc.sync.dma_start(l5[:], offs5)
        nc.sync.dma_start(out=vs_w[:].bitcast(I32), in_=vs_words[0].bitcast(I32))

        def deal(dst, src):
            nc.vector.tensor_copy(dst.rearrange("p (t m) -> p t m", t=PACK), src.rearrange("p (m t) -> p t m", t=PACK))

        deal(w_p[:, 0:R], w_raw[:, 0:R])
        deal(ws_p[:, 0:R], ws_raw[:, 0:R])
        deal(w_p[:, R:2 * R], w_raw[:, R:2 * R])
        nc.vector.tensor_copy(xtg_w[:], xt_w[:].indirect(l1[:]))
        nc.vector.tensor_copy(xtg_s[:], xt_s[:].indirect(l1[:]))
        nc.vector.tensor_copy(xog_w[:], xo_w[:].indirect(l2[:]))
        deal(ws_p[:, R:2 * R], ws_raw[:, R:2 * R])
        nc.vector.tensor_copy(xog_s[:], xo_s[:].indirect(l2[:]))

        acc = [ps.tile([P, J], F32, name="acc%d" % t) for t in range(PACK)]
        for t in range(PACK):
            c0 = slice(t * P, (t + 1) * P)
            nc.tensor.matmul_mx(out=acc[t][:], lhsT=w_p[:, c0].bitcast(E2M1), lhsT_scale=ws_p[:, c0],
                                rhs=xtg_w[:].bitcast(E5M2), rhs_scale=xtg_s[:], start=True, stop=False)
        for t in range(PACK):
            c1 = slice(R + t * P, R + (t + 1) * P)
            nc.tensor.matmul_mx(out=acc[t][:], lhsT=w_p[:, c1].bitcast(E2M1), lhsT_scale=ws_p[:, c1],
                                rhs=xog_w[:].bitcast(E4M3), rhs_scale=xog_s[:], start=False, stop=True)


        a_sb = [tile("a_sb%d" % t, [P, J], F32) for t in range(PACK)]
        for t in range(PACK):
            if t == 0:
                nc.vector.tensor_copy(a_sb[t][:], acc[t][:])
            else:
                nc.scalar.copy(a_sb[t][:], acc[t][:])
        nc.vector.tensor_copy(pw[0][:].indirect(l3[:]), a_sb[0][:])
        for t in range(1, PACK):
            nc.scalar.activation(pw[t][:].indirect(l3[:]), a_sb[t][:], ACT.Copy)
        nc.vector.tensor_copy(vsg_s[:], vs_s[:].indirect(l6[:]))

        dif = [tile("dif%d" % t, [P, C], F32) for t in range(PACK)]
        pg = [tile("pg%d" % t, [P, C], F32) for t in range(PACK)]
        for t in range(PACK - 1):
            nc.vector.tensor_tensor(dif[t][:], tbt[t][:].indirect(l4[:]), pw[t][:], ALU.subtract)
            nc.scalar.activation(pg[t][:], dif[t][:], ACT.Abs)
        for g in range(2):
            cols = slice(g * C // 2, (g + 1) * C // 2)
            nc.vector.tensor_tensor(dif[3][:, cols], tbt[3][:].indirect(l4[:, 16 * g:16 * g + 16]), pw[3][:, cols], ALU.subtract)
            nc.scalar.activation(pg[3][:, cols], dif[3][:, cols], ACT.Abs)
        nc.vector.tensor_copy(vsg_w[:], vs_w[:].indirect(l6[:]))
        for t in (0, 1):
            nc.scalar.activation(hid[:, t, :], pg[t][:].indirect(l5[:]), ACT.Copy)
        nc.vector.tensor_copy(hid[:, 2, :], pg[2][:].indirect(l5[:]))
        nc.vector.tensor_copy(hid[:, 3, 0:P], pg[3][:].indirect(l5[:, 0:8]))
        nc.scalar.activation(hid[:, 3, P:O], pg[3][:].indirect(l5[:, 8:16]), ACT.Copy)

        hid_bf = [tile("hid_bf%d" % g, [P, P, PACK], BF16) for g in range(2)]
        hid_w = [tile("hid_w%d" % g, [P, P], U32) for g in range(2)]
        hid_s = [tile("hid_s%d" % g, [P, P], U8) for g in range(2)]
        for g in range(2):
            nc.vector.tensor_copy(hid_bf[g][:].rearrange("p (c i) t -> p c t i", i=4),
                                  hid[:, :, g * P:(g + 1) * P].rearrange("p t (c i) -> p c t i", i=4))
        for g in range(2):
            nc.vector.quantize_mx(out=hid_w[g][:].bitcast(E4M3), scales=hid_s[g][:],
                                  in_=hid_bf[g][:].rearrange("p o t -> p (o t)"))
        for g in range(2):
            for h in range(2):
                rows = slice(h * P, (h + 1) * P)
                y = ps.tile([P, P], F32, name="y%d%d" % (g, h))
                nc.tensor.matmul_mx(out=y[:], lhsT=vsg_w[:, rows].bitcast(E2M1), lhsT_scale=vsg_s[:, rows],
                                    rhs=hid_w[g][:].bitcast(E4M3), rhs_scale=hid_s[g][:], start=True, stop=True)
                y_sb = tile("y_sb%d%d" % (g, h), [P, P], F32)
                if g == 1 and h == 0:
                    nc.vector.tensor_copy(y_sb[:], y[:])
                else:
                    nc.scalar.copy(y_sb[:], y[:])
                queue = nc.scalar if g == 1 and h == 1 else nc.sync
                queue.dma_start(out=out[rows, g * P:(g + 1) * P], in_=y_sb[:])
